import numpy as np
import ml_dtypes


def mxq(x, axis, fmt="e4m3"):
    dtype, down = {"e4m3": (ml_dtypes.float8_e4m3fn, 7), "e5m2": (ml_dtypes.float8_e5m2, 14)}[fmt]
    v = np.moveaxis(np.asarray(x, np.float32).astype(ml_dtypes.bfloat16).astype(np.float64), axis, -1)
    blocks = v.reshape(v.shape[:-1] + (-1, 32))
    amax = np.abs(blocks).max(-1, keepdims=True)
    byte = np.maximum(np.where(amax > 0, np.frexp(amax)[1] - 1 + 127, 0) - down, 1)
    scale = np.exp2(byte - 127.0)
    codes = (blocks / scale).astype(np.float32).astype(dtype).astype(np.float64)
    return np.moveaxis((codes * scale).reshape(v.shape), -1, axis)


WIDE = False


def mx_kscale(k):
    if not WIDE:
        return np.ones(k)
    levels = np.array([10, -10, 5, -5, 0])
    if k % 512:
        return np.exp2(np.random.permutation(np.resize(levels, k // 32))).repeat(32)
    a = np.empty((k // 512, 16))
    for p in range(k // 512):
        a[p, :8] = np.random.permutation(np.resize(levels, 8))
        for g in range(8):
            far = levels[np.abs(levels - a[p, g]) >= 10]
            a[p, g + 8] = far[np.random.randint(len(far))]
    return np.exp2(a.ravel()).repeat(32)


BF16 = ml_dtypes.bfloat16


def bf(x):
    return np.asarray(x, np.float32).astype(BF16)


def f64(x):
    return np.asarray(x).astype(np.float64)


N, D, H = 1024, 1024, 512
G = 2 * H


def sigmoid(v):
    return 1.0 / (1.0 + np.exp(-v))


def mogrify(x, h, q):
    a = h @ q
    return 2.0 * sigmoid(a) * x


def draw0():
    t = mx_kscale(D)
    return {
        "x": bf(np.random.standard_normal((N, D)) * t),
        "h": bf(np.random.standard_normal((N, H))),
        "c": bf(np.random.standard_normal((N, H))),
        "q": bf(np.random.standard_normal((H, D)) / np.sqrt(H)),
        "w": bf(np.random.standard_normal((D, G)) / np.sqrt(D) / t[:, None]),
        "u": bf(np.random.standard_normal((H, G)) / np.sqrt(H)),
        "b": bf(np.random.standard_normal(G) * 0.3),
    }


def core(x, h, c, q, w, u, b):
    hidden = h.shape[1]
    x1 = mogrify(f64(x), f64(h), f64(q))
    pre = (mxq(x1, 1, "e4m3") @ mxq(f64(w), 0, "e4m3")) + f64(h) @ f64(u) + f64(b)
    pi = pre[:, 0:hidden]
    pg = pre[:, hidden:2 * hidden]
    i = sigmoid(pi)
    g = np.tanh(pg)
    return (1.0 - i) * f64(c) + i * g


def e4m3fn_bytes(y):
    return np.clip(np.asarray(y, np.float64), -448.0, 448.0).astype(np.float32).astype(ml_dtypes.float8_e4m3fn).view(np.uint8)


def e4m3fn_values(b):
    return np.asarray(b, np.uint8).view(ml_dtypes.float8_e4m3fn).astype(np.float64)


def setup_inputs():
    d = draw0()
    x0 = np.asarray(d['w']).astype(np.float64)
    s = (np.max(np.abs(x0), axis=(1,), keepdims=True) / 448.0).astype(np.float32)
    out = {}
    for k, v in d.items():
        if k == 'w':
            out['w_bytes'] = e4m3fn_bytes(x0 / s.astype(np.float64))
            out['w_scale'] = s
        else:
            out[k] = v
    return out


def reference(x, h, c, q, w_bytes, w_scale, u, b):
    return core(x, h, c, q, e4m3fn_values(w_bytes) * w_scale.astype(np.float64), u, b)

@@ -1,0 +1,403 @@
+from contextlib import ExitStack
+
+import concourse.mybir as mybir
+from concourse.masks import make_identity
+
+F32 = mybir.dt.float32
+BF16 = mybir.dt.bfloat16
+U32 = mybir.dt.uint32
+U8 = mybir.dt.uint8
+FP8 = mybir.dt.float8_e4m3fn
+FP8X4 = mybir.dt.float8_e4m3fn_x4
+ACT = mybir.ActivationFunctionType
+ALU = mybir.AluOpType
+
+N, D, H = 1024, 1024, 512
+G = 2 * H
+P = 128
+PACK = 4
+HALVES = 2
+HALF = N // HALVES
+TILES = HALF // P
+PASSES = D // (P * PACK)
+KC = H // P
+BANK = 512
+
+FLOPS = 2 * N * H * D + 2 * N * H * G + 2 * N * D * G
+
+
+def tile_mogrifieroneroundcoupledlstmcell_kernel(tc, x, h, c, q, w_bytes, w_scale, u, b, out):
+    nc = tc.nc
+    with ExitStack() as ctx:
+        keep = ctx.enter_context(tc.tile_pool(name="keep", bufs=1))
+        work = ctx.enter_context(tc.tile_pool(name="work", bufs=1))
+        ring = ctx.enter_context(tc.psum_pool(name="ring", bufs=1))
+        counts = {}
+
+        def turn(name, length):
+            counts[name] = counts.get(name, -1) + 1
+            return f"{name}_{counts[name] % length}"
+
+        ident16 = keep.tile([P, P], BF16, name="ident16")
+        make_identity(nc, ident16[:])
+        ident32 = keep.tile([P, P], F32, name="ident32")
+        make_identity(nc, ident32[:])
+
+        ctx.enter_context(tc.manual_schedule())
+
+        idle = keep.tile([P, BANK], BF16, name="idle")
+        nc.vector.memset(idle[:], 0.0)
+        scratch = keep.tile([P, 1], F32, name="scratch")
+        nc.vector.memset(scratch[:], 0.0)
+        brow = keep.tile([P, G], BF16, name="brow")
+        nc.vector.memset(brow[:], 0.0)
+        ones = keep.tile([P, P], BF16, name="ones")
+        nc.vector.memset(ones[:], 1.0)
+        for k in range(4):
+            bank = ring.tile([P, BANK], F32, name="bank_7")
+            nc.tensor.matmul(bank[:], lhsT=idle[:, 0:P], rhs=idle[:], start=True, stop=True)
+
+        hv = h.rearrange("(s p j) k -> s p j k", s=HALVES, p=P)
+        xv = x.rearrange("(s p j) k -> s p j k", s=HALVES, p=P)
+        cv = c.rearrange("(s p j) k -> s p j k", s=HALVES, p=P)
+        ov = out.rearrange("(s p j) k -> s p j k", s=HALVES, p=P)
+        qv = q.rearrange("(kc p) d -> p kc d", p=P)
+        uv = u.rearrange("(kc p) n -> p kc n", p=P)
+        wv = w_bytes.rearrange("(g p t) n -> g p t n", p=P, t=PACK)
+        sv = w_scale.rearrange("(g p t) o -> p g (t o)", p=P, t=PACK)
+
+        h_sb, x_sb, c_sb, w_by = [], [], [], []
+        for s in range(HALVES):
+            h_half = keep.tile([P, TILES, H], BF16, name=f"h{s}")
+            h_sb.append(h_half)
+            x_half = keep.tile([P, TILES, D], BF16, name=f"x{s}")
+            x_sb.append(x_half)
+            c_half = keep.tile([P, TILES, H], BF16, name=f"c{s}")
+            c_sb.append(c_half)
+        for g in range(PASSES):
+            w_half = keep.tile([P, PACK, G], U8, name=f"wb{g}")
+            w_by.append(w_half)
+        q_sb = keep.tile([P, KC, D], BF16, name="q_sb")
+        u_sb = keep.tile([P, KC, G], BF16, name="u_sb")
+        w_sc = keep.tile([P, PASSES, PACK], F32, name="w_sc")
+
+        nc.scalar.dma_start(out=w_sc[:], in_=sv)
+        nc.scalar.dma_start(out=brow[0:1, :], in_=b.rearrange("(o n) -> o n", o=1))
+        nc.scalar.activation(out=scratch[:], in_=scratch[:], func=ACT.Sigmoid)
+        for j in range(0, TILES, 2):
+            nc.sync.dma_start(out=h_sb[0][:, j : j + 2, :], in_=hv[0][:, j : j + 2, :])
+        nc.sync.dma_start(out=q_sb[:, :, 0:BANK], in_=qv[:, :, 0:BANK])
+        nc.sync.dma_start(out=w_by[0][:], in_=wv[0])
+        nc.sync.dma_start(out=x_sb[0][:], in_=xv[0])
+        nc.sync.dma_start(out=q_sb[:, :, BANK:D], in_=qv[:, :, BANK:D])
+        nc.sync.dma_start(out=h_sb[1][:], in_=hv[1])
+        nc.sync.dma_start(out=w_by[1][:], in_=wv[1])
+        nc.sync.dma_start(out=x_sb[1][:], in_=xv[1])
+        nc.sync.dma_start(out=u_sb[:], in_=uv)
+        for s in range(HALVES):
+            nc.sync.dma_start(out=c_sb[s][:], in_=cv[s])
+
+        hT, xw, sig, x1, xq, xs = [], [], {}, {}, {}, {}
+        for s in range(HALVES):
+            hT_half = keep.tile([P, KC, HALF], BF16, name=f"hT{s}")
+            hT.append(hT_half)
+            xw_half = keep.tile([P, TILES, PASSES, 2, P], F32, name=f"xw{s}")
+            xw.append(xw_half)
+            for g in range(PASSES):
+                sig_t = keep.tile([P, PACK, HALF], F32, name=f"sig{s}{g}")
+                sig[s, g] = sig_t
+                x1_t = keep.tile([P, HALF, PACK], BF16, name=f"x1_{s}{g}", align_bytes=64)
+                x1[s, g] = x1_t
+                xq_t = keep.tile([P, HALF], U32, name=f"xq{s}{g}", align_bytes=64)
+                xq[s, g] = xq_t
+                xs_t = keep.tile([P, HALF], U8, name=f"xs{s}{g}", align_bytes=64)
+                xs[s, g] = xs_t
+        wide, wi, wq, ws = [], [], [], []
+        for g in range(PASSES):
+            wide_t = keep.tile([P, PACK, G], BF16, name=f"wide{g}")
+            wide.append(wide_t)
+            wi_t = keep.tile([P, G, PACK], BF16, name=f"wi{g}", align_bytes=64)
+            wi.append(wi_t)
+            wq_t = keep.tile([P, G], U32, name=f"wq{g}", align_bytes=64)
+            wq.append(wq_t)
+            ws_t = keep.tile([P, G], U8, name=f"ws{g}", align_bytes=64)
+            ws.append(ws_t)
+        bias = keep.tile([P, BANK], F32, name="bias")
+
+        def turn_h(i, engine):
+            s, j = divmod(i, TILES)
+            bank = ring.tile([P, KC, P], BF16, name=turn("bank", 8))
+            for kc in range(KC):
+                nc.tensor.transpose(bank[:, kc, :], h_sb[s][:, j, kc * P : (kc + 1) * P], ident16[:])
+            engine(out=hT[s][:, :, j * P : (j + 1) * P], in_=bank[:])
+
+        def gate_logits(s, g, t):
+            bank = ring.tile([P, BANK], F32, name=turn("bank", 8))
+            for kc in range(KC):
+                nc.tensor.matmul(
+                    bank[:],
+                    lhsT=q_sb[:, kc, g * BANK + t : (g + 1) * BANK : PACK],
+                    rhs=hT[s][:, kc, :],
+                    start=(kc == 0),
+                    stop=(kc == KC - 1),
+                )
+            nc.scalar.activation(out=sig[s, g][:, t, :], in_=bank[:], func=ACT.Sigmoid)
+
+        def order_x(s, g):
+            words = x_sb[s][:].bitcast(F32).rearrange("p j (g m u) -> p j g u m", g=PASSES, u=2)
+            nc.scalar.copy(out=xw[s][:, :, g, :, :], in_=words[:, :, g, :, :])
+
+        xbank = {}
+
+        def turn_x(s, g):
+            for pr in range(2):
+                bank = ring.tile([P, 2, 2 * P], F32, name=turn("bank", 8))
+                for jj in range(2):
+                    for v in range(2):
+                        nc.tensor.transpose(
+                            bank[:, v, jj * P : (jj + 1) * P], xw[s][:, 2 * pr + jj, g, v, :], ident32[:]
+                        )
+                xbank[s, g, pr] = bank
+
+        def gate_x(s, g, pr):
+            n = slice(pr * 2 * P, (pr + 1) * 2 * P)
+            nc.vector.tensor_tensor(
+                out=x1[s, g][:, n, :].rearrange("p n (u e) -> p n u e", u=2),
+                in0=sig[s, g][:, :, n].rearrange("p (u e) n -> p n u e", u=2),
+                in1=xbank[s, g, pr][:].bitcast(BF16).rearrange("p u (n e) -> p n u e", e=2),
+                op=ALU.mult,
+            )
+
+        def quantize_x(s, g):
+            nc.vector.quantize_mx(
+                out=xq[s, g][:].bitcast(FP8X4),
+                scales=xs[s, g][:],
+                in_=x1[s, g][:].rearrange("p n t -> p (n t)"),
+            )
+
+        def widen_v(g, t):
+            nc.vector.tensor_scalar(
+                out=wide[g][:, t, :],
+                in0=w_by[g][:, t, :].bitcast(FP8),
+                scalar1=w_sc[:, g, t : t + 1],
+                scalar2=None,
+                op0=ALU.mult,
+            )
+
+        def widen_s(g, t):
+            nc.scalar.activation(
+                out=wide[g][:, t, :],
+                in_=w_by[g][:, t, :].bitcast(FP8),
+                func=ACT.Copy,
+                scale=w_sc[:, g, t : t + 1],
+            )
+
+        def interleave_w(g, j):
+            n = slice(j * BANK, (j + 1) * BANK)
+            nc.vector.tensor_copy(out=wi[g][:, n, :], in_=wide[g][:, :, n].rearrange("p t n -> p n t"))
+
+        def quantize_w(g, j):
+            n = slice(j * BANK, (j + 1) * BANK)
+            nc.vector.quantize_mx(
+                out=wq[g][:, n].bitcast(FP8X4),
+                scales=ws[g][:, n],
+                in_=wi[g][:, n, :].rearrange("p n t -> p (n t)"),
+            )
+
+        def spread_bias():
+            bank = ring.tile([P, BANK], F32, name=turn("bank", 8))
+            nc.tensor.matmul(bank[:], lhsT=ones[:], rhs=brow[:, BANK:G], start=True, stop=True)
+            nc.scalar.copy(out=bias[:], in_=bank[:])
+
+        hub, hubank = {}, {}
+
+        def hidden(i):
+            s, j = divmod(i, TILES)
+            for k in (1, 0):
+                bank = ring.tile([P, BANK], F32, name=turn("bank", 8))
+                if k == 0:
+                    nc.tensor.matmul(bank[:], lhsT=ones[:], rhs=brow[:, 0:BANK], start=True, stop=False)
+                for kc in range(KC):
+                    nc.tensor.matmul(
+                        bank[:],
+                        lhsT=hT[s][:, kc, j * P : (j + 1) * P],
+                        rhs=u_sb[:, kc, k * BANK : (k + 1) * BANK],
+                        start=(kc == 0 and k == 1),
+                        stop=(kc == KC - 1),
+                    )
+                hubank[i, k] = bank
+
+        def keep_hidden(i, k):
+            hub_t = work.tile([P, BANK], F32, name=turn(f"hub{k}", 4))
+            hub[i, k] = hub_t
+            if k == 1:
+                nc.vector.tensor_tensor(out=hub_t[:], in0=hubank[i, k][:], in1=bias[:], op=ALU.add)
+            else:
+                nc.scalar.copy(out=hub_t[:], in_=hubank[i, k][:])
+
+        mxbank = {}
+
+        def product(i):
+            s, j = divmod(i, TILES)
+            for k in (1, 0):
+                bank = ring.tile([P, BANK], F32, name=turn("bank", 8))
+                for g in range(PASSES):
+                    nc.tensor.matmul_mx(
+                        out=bank[:],
+                        lhsT=xq[s, g][:, j * P : (j + 1) * P].bitcast(FP8X4),
+                        lhsT_scale=xs[s, g][:, j * P : (j + 1) * P],
+                        rhs=wq[g][:, k * BANK : (k + 1) * BANK].bitcast(FP8X4),
+                        rhs_scale=ws[g][:, k * BANK : (k + 1) * BANK],
+                        start=(g == 0),
+                        stop=(g == PASSES - 1),
+                    )
+                mxbank[i, k] = bank
+
+        pre, act, low = {}, {}, {}
+
+        def add_up(i, k, n=slice(0, BANK)):
+            if (i, k) not in pre:
+                pre_t = work.tile([P, BANK], F32, name=turn(f"pre{k}", 4))
+                pre[i, k] = pre_t
+                act[i, k] = pre_t
+            nc.vector.scalar_tensor_tensor(
+                out=pre[i, k][:, n], in0=mxbank[i, k][:, n], scalar=2.0, in1=hub[i, k][:, n], op0=ALU.mult, op1=ALU.add
+            )
+            nc.scalar.activation(
+                out=act[i, k][:, n], in_=pre[i, k][:, n], func=(ACT.Tanh if k else ACT.Sigmoid)
+            )
+
+        def differ(i):
+            s, j = divmod(i, TILES)
+            low_t = work.tile([P, BANK], F32, name=turn("low", 4))
+            low[i] = low_t
+            nc.vector.tensor_tensor(out=low_t[:], in0=act[i, 1][:], in1=c_sb[s][:, j, :], op=ALU.subtract)
+
+        def weigh(i, n=slice(0, BANK)):
+            nc.vector.tensor_tensor(out=low[i][:, n], in0=low[i][:, n], in1=act[i, 0][:, n], op=ALU.mult)
+
+        def finish(i, n=slice(0, BANK)):
+            s, j = divmod(i, TILES)
+            nc.vector.tensor_tensor(out=low[i][:, n], in0=low[i][:, n], in1=c_sb[s][:, j, n], op=ALU.add)
+            nc.sync.dma_start(out=ov[s][:, j, n], in_=low[i][:, n])
+
+        vcopy, scopy = nc.vector.tensor_copy, nc.scalar.copy
+
+        def turn_half(s):
+            for j in range(TILES):
+                turn_h(s * TILES + j, vcopy if j % 2 == 0 else scopy)
+
+        spread_bias()
+        turn_half(0)
+        for t in range(PACK):
+            widen_v(0, t)
+        for t in range(PACK):
+            gate_logits(0, 0, t)
+            if t == 1:
+                order_x(0, 0)
+        for j in range(2):
+            interleave_w(0, j)
+        for j in range(2):
+            quantize_w(0, j)
+        order_x(0, 1)
+        for t in range(PACK):
+            gate_logits(0, 1, t)
+            if t == 1:
+                widen_s(1, 2)
+        widen_s(1, 3)
+        turn_x(0, 0)
+        widen_v(1, 0)
+        widen_v(1, 1)
+        gate_x(0, 0, 0)
+        turn_half(1)
+        turn_x(0, 1)
+        order_x(1, 0)
+        order_x(1, 1)
+        gate_x(0, 0, 1)
+        gate_x(0, 1, 0)
+        gate_x(0, 1, 1)
+        for t in range(PACK):
+            gate_logits(1, 0, t)
+        interleave_w(1, 0)
+        interleave_w(1, 1)
+        quantize_x(0, 0)
+        quantize_x(0, 1)
+        quantize_w(1, 1)
+        quantize_w(1, 0)
+
+        def keep_pair(i):
+            for m in (i, i + 1):
+                keep_hidden(m, 1)
+                keep_hidden(m, 0)
+
+        hidden(0)
+        hidden(1)
+        keep_pair(0)
+        product(0)
+        product(1)
+        turn_x(1, 0)
+        for i in (0, 1):
+            add_up(i, 1)
+            add_up(i, 0)
+        gate_x(1, 0, 0)
+        gate_x(1, 0, 1)
+        differ(0)
+        quantize_x(1, 0)
+        differ(1)
+        for t in range(PACK):
+            gate_logits(1, 1, t)
+        turn_x(1, 1)
+        weigh(0)
+        weigh(1)
+        finish(0)
+        gate_x(1, 1, 0)
+        gate_x(1, 1, 1)
+        hidden(2)
+        keep_hidden(2, 1)
+        keep_hidden(2, 0)
+        quantize_x(1, 1)
+        finish(1)
+        hidden(3)
+        keep_hidden(3, 1)
+        keep_hidden(3, 0)
+        for i in (2, 4):
+            product(i)
+            product(i + 1)
+            for m in (i, i + 1):
+                add_up(m, 1)
+                add_up(m, 0)
+            hidden(i + 2)
+            differ(i)
+            keep_hidden(i + 2, 1)
+            keep_hidden(i + 2, 0)
+            differ(i + 1)
+            weigh(i)
+            if i == 2:
+                weigh(i + 1)
+                hidden(i + 3)
+                keep_hidden(i + 3, 1)
+                keep_hidden(i + 3, 0)
+                finish(i)
+                finish(i + 1)
+        product(6)
+        add_up(6, 1)
+        add_up(6, 0)
+        weigh(5)
+        hidden(7)
+        keep_hidden(7, 1)
+        keep_hidden(7, 0)
+        differ(6)
+        finish(4)
+        finish(5)
+        product(7)
+        lo, hi = slice(0, BANK // 2), slice(BANK // 2, BANK)
+        add_up(7, 1)
+        add_up(7, 0, lo)
+        add_up(7, 0, hi)
+        weigh(6)
+        differ(7)
+        finish(6)
+        weigh(7, lo)
+        weigh(7, hi)
+        finish(7, lo)
+        finish(7, hi)

@@ -22,6 +22,7 @@ TILES = HALF // P
 PASSES = D // (P * PACK)
 KC = H // P
 BANK = 512
+SCALAR_TILES = (7,)
 
 FLOPS = 2 * N * H * D + 2 * N * H * G + 2 * N * D * G
 
@@ -77,19 +78,22 @@ def tile_mogrifieroneroundcoupledlstmcell_kernel(tc, x, h, c, q, w_bytes, w_scal
         for g in range(PASSES):
             w_half = keep.tile([P, PACK, G], U8, name=f"wb{g}")
             w_by.append(w_half)
-        q_sb = keep.tile([P, KC, D], BF16, name="q_sb")
+        q_sb = []
+        for g in range(PASSES):
+            q_half = keep.tile([P, KC, BANK], BF16, name=f"q{g}")
+            q_sb.append(q_half)
         u_sb = keep.tile([P, KC, G], BF16, name="u_sb")
         w_sc = keep.tile([P, PASSES, PACK], F32, name="w_sc")
 
-        nc.scalar.dma_start(out=w_sc[:], in_=sv)
-        nc.scalar.dma_start(out=brow[0:1, :], in_=b.rearrange("(o n) -> o n", o=1))
         nc.scalar.activation(out=scratch[:], in_=scratch[:], func=ACT.Sigmoid)
         for j in range(0, TILES, 2):
             nc.sync.dma_start(out=h_sb[0][:, j : j + 2, :], in_=hv[0][:, j : j + 2, :])
-        nc.sync.dma_start(out=q_sb[:, :, 0:BANK], in_=qv[:, :, 0:BANK])
+        nc.sync.dma_start(out=q_sb[0][:], in_=qv[:, :, 0:BANK])
+        nc.sync.dma_start(out=w_sc[:], in_=sv)
         nc.sync.dma_start(out=w_by[0][:], in_=wv[0])
+        nc.sync.dma_start(out=brow[0:1, :], in_=b.rearrange("(o n) -> o n", o=1))
         nc.sync.dma_start(out=x_sb[0][:], in_=xv[0])
-        nc.sync.dma_start(out=q_sb[:, :, BANK:D], in_=qv[:, :, BANK:D])
+        nc.sync.dma_start(out=q_sb[1][:], in_=qv[:, :, BANK:D])
         nc.sync.dma_start(out=h_sb[1][:], in_=hv[1])
         nc.sync.dma_start(out=w_by[1][:], in_=wv[1])
         nc.sync.dma_start(out=x_sb[1][:], in_=xv[1])
@@ -97,15 +101,15 @@ def tile_mogrifieroneroundcoupledlstmcell_kernel(tc, x, h, c, q, w_bytes, w_scal
         for s in range(HALVES):
             nc.sync.dma_start(out=c_sb[s][:], in_=cv[s])
 
-        hT, xw, sig, x1, xq, xs = [], [], {}, {}, {}, {}
+        hT, xw, sig, x1, xq, xs = [], {}, {}, {}, {}, {}
         for s in range(HALVES):
-            hT_half = keep.tile([P, KC, HALF], BF16, name=f"hT{s}")
+            hT_half = keep.tile([P, TILES, KC, P], BF16, name=f"hT{s}")
             hT.append(hT_half)
-            xw_half = keep.tile([P, TILES, PASSES, 2, P], F32, name=f"xw{s}")
-            xw.append(xw_half)
             for g in range(PASSES):
                 sig_t = keep.tile([P, PACK, HALF], F32, name=f"sig{s}{g}")
                 sig[s, g] = sig_t
+                xw_t = keep.tile([P, TILES, 2, P], F32, name=f"xw{s}{g}")
+                xw[s, g] = xw_t
                 x1_t = keep.tile([P, HALF, PACK], BF16, name=f"x1_{s}{g}", align_bytes=64)
                 x1[s, g] = x1_t
                 xq_t = keep.tile([P, HALF], U32, name=f"xq{s}{g}", align_bytes=64)
@@ -129,15 +133,15 @@ def tile_mogrifieroneroundcoupledlstmcell_kernel(tc, x, h, c, q, w_bytes, w_scal
             bank = ring.tile([P, KC, P], BF16, name=turn("bank", 8))
             for kc in range(KC):
                 nc.tensor.transpose(bank[:, kc, :], h_sb[s][:, j, kc * P : (kc + 1) * P], ident16[:])
-            engine(out=hT[s][:, :, j * P : (j + 1) * P], in_=bank[:])
+            engine(out=hT[s][:, j, :, :], in_=bank[:])
 
         def gate_logits(s, g, t):
             bank = ring.tile([P, BANK], F32, name=turn("bank", 8))
             for kc in range(KC):
                 nc.tensor.matmul(
                     bank[:],
-                    lhsT=q_sb[:, kc, g * BANK + t : (g + 1) * BANK : PACK],
-                    rhs=hT[s][:, kc, :],
+                    lhsT=q_sb[g][:, kc, t:BANK:PACK],
+                    rhs=hT[s][:, :, kc, :],
                     start=(kc == 0),
                     stop=(kc == KC - 1),
                 )
@@ -145,7 +149,7 @@ def tile_mogrifieroneroundcoupledlstmcell_kernel(tc, x, h, c, q, w_bytes, w_scal
 
         def order_x(s, g):
             words = x_sb[s][:].bitcast(F32).rearrange("p j (g m u) -> p j g u m", g=PASSES, u=2)
-            nc.scalar.copy(out=xw[s][:, :, g, :, :], in_=words[:, :, g, :, :])
+            nc.scalar.copy(out=xw[s, g][:], in_=words[:, :, g, :, :])
 
         xbank = {}
 
@@ -155,7 +159,7 @@ def tile_mogrifieroneroundcoupledlstmcell_kernel(tc, x, h, c, q, w_bytes, w_scal
                 for jj in range(2):
                     for v in range(2):
                         nc.tensor.transpose(
-                            bank[:, v, jj * P : (jj + 1) * P], xw[s][:, 2 * pr + jj, g, v, :], ident32[:]
+                            bank[:, v, jj * P : (jj + 1) * P], xw[s, g][:, 2 * pr + jj, v, :], ident32[:]
                         )
                 xbank[s, g, pr] = bank
 
@@ -215,14 +219,17 @@ def tile_mogrifieroneroundcoupledlstmcell_kernel(tc, x, h, c, q, w_bytes, w_scal
             s, j = divmod(i, TILES)
             for k in (1, 0):
                 bank = ring.tile([P, BANK], F32, name=turn("bank", 8))
-                if k == 0:
-                    nc.tensor.matmul(bank[:], lhsT=ones[:], rhs=brow[:, 0:BANK], start=True, stop=False)
+                biased = k == 0 or i in SCALAR_TILES
+                if biased:
+                    nc.tensor.matmul(
+                        bank[:], lhsT=ones[:], rhs=brow[:, k * BANK : (k + 1) * BANK], start=True, stop=False
+                    )
                 for kc in range(KC):
                     nc.tensor.matmul(
                         bank[:],
-                        lhsT=hT[s][:, kc, j * P : (j + 1) * P],
+                        lhsT=hT[s][:, j, kc, :],
                         rhs=u_sb[:, kc, k * BANK : (k + 1) * BANK],
-                        start=(kc == 0 and k == 1),
+                        start=(kc == 0 and not biased),
                         stop=(kc == KC - 1),
                     )
                 hubank[i, k] = bank
@@ -230,28 +237,28 @@ def tile_mogrifieroneroundcoupledlstmcell_kernel(tc, x, h, c, q, w_bytes, w_scal
         def keep_hidden(i, k):
             hub_t = work.tile([P, BANK], F32, name=turn(f"hub{k}", 4))
             hub[i, k] = hub_t
-            if k == 1:
+            if k == 1 and i not in SCALAR_TILES:
                 nc.vector.tensor_tensor(out=hub_t[:], in0=hubank[i, k][:], in1=bias[:], op=ALU.add)
             else:
                 nc.scalar.copy(out=hub_t[:], in_=hubank[i, k][:])
 
         mxbank = {}
 
-        def product(i):
+        def product(i, k, n=slice(0, BANK)):
             s, j = divmod(i, TILES)
-            for k in (1, 0):
-                bank = ring.tile([P, BANK], F32, name=turn("bank", 8))
-                for g in range(PASSES):
-                    nc.tensor.matmul_mx(
-                        out=bank[:],
-                        lhsT=xq[s, g][:, j * P : (j + 1) * P].bitcast(FP8X4),
-                        lhsT_scale=xs[s, g][:, j * P : (j + 1) * P],
-                        rhs=wq[g][:, k * BANK : (k + 1) * BANK].bitcast(FP8X4),
-                        rhs_scale=ws[g][:, k * BANK : (k + 1) * BANK],
-                        start=(g == 0),
-                        stop=(g == PASSES - 1),
-                    )
-                mxbank[i, k] = bank
+            cols = slice(k * BANK + n.start, k * BANK + n.stop)
+            bank = ring.tile([P, n.stop - n.start], F32, name=turn("bank", 8))
+            for g in range(PASSES):
+                nc.tensor.matmul_mx(
+                    out=bank[:],
+                    lhsT=xq[s, g][:, j * P : (j + 1) * P].bitcast(FP8X4),
+                    lhsT_scale=xs[s, g][:, j * P : (j + 1) * P],
+                    rhs=wq[g][:, cols].bitcast(FP8X4),
+                    rhs_scale=ws[g][:, cols],
+                    start=(g == 0),
+                    stop=(g == PASSES - 1),
+                )
+            mxbank[i, k, n.start] = bank
 
         pre, act, low = {}, {}, {}
 
@@ -261,7 +268,7 @@ def tile_mogrifieroneroundcoupledlstmcell_kernel(tc, x, h, c, q, w_bytes, w_scal
                 pre[i, k] = pre_t
                 act[i, k] = pre_t
             nc.vector.scalar_tensor_tensor(
-                out=pre[i, k][:, n], in0=mxbank[i, k][:, n], scalar=2.0, in1=hub[i, k][:, n], op0=ALU.mult, op1=ALU.add
+                out=pre[i, k][:, n], in0=mxbank[i, k, n.start][:], scalar=2.0, in1=hub[i, k][:, n], op0=ALU.mult, op1=ALU.add
             )
             nc.scalar.activation(
                 out=act[i, k][:, n], in_=pre[i, k][:, n], func=(ACT.Tanh if k else ACT.Sigmoid)
@@ -287,7 +294,6 @@ def tile_mogrifieroneroundcoupledlstmcell_kernel(tc, x, h, c, q, w_bytes, w_scal
             for j in range(TILES):
                 turn_h(s * TILES + j, vcopy if j % 2 == 0 else scopy)
 
-        spread_bias()
         turn_half(0)
         for t in range(PACK):
             widen_v(0, t)
@@ -305,6 +311,7 @@ def tile_mogrifieroneroundcoupledlstmcell_kernel(tc, x, h, c, q, w_bytes, w_scal
             if t == 1:
                 widen_s(1, 2)
         widen_s(1, 3)
+        spread_bias()
         turn_x(0, 0)
         widen_v(1, 0)
         widen_v(1, 1)
@@ -333,8 +340,10 @@ def tile_mogrifieroneroundcoupledlstmcell_kernel(tc, x, h, c, q, w_bytes, w_scal
         hidden(0)
         hidden(1)
         keep_pair(0)
-        product(0)
-        product(1)
+        product(0, 1)
+        product(0, 0)
+        product(1, 1)
+        product(1, 0)
         turn_x(1, 0)
         for i in (0, 1):
             add_up(i, 1)
@@ -361,8 +370,10 @@ def tile_mogrifieroneroundcoupledlstmcell_kernel(tc, x, h, c, q, w_bytes, w_scal
         keep_hidden(3, 1)
         keep_hidden(3, 0)
         for i in (2, 4):
-            product(i)
-            product(i + 1)
+            product(i, 1)
+            product(i, 0)
+            product(i + 1, 1)
+            product(i + 1, 0)
             for m in (i, i + 1):
                 add_up(m, 1)
                 add_up(m, 0)
@@ -379,7 +390,8 @@ def tile_mogrifieroneroundcoupledlstmcell_kernel(tc, x, h, c, q, w_bytes, w_scal
                 keep_hidden(i + 3, 0)
                 finish(i)
                 finish(i + 1)
-        product(6)
+        product(6, 1)
+        product(6, 0)
         add_up(6, 1)
         add_up(6, 0)
         weigh(5)
@@ -389,14 +401,16 @@ def tile_mogrifieroneroundcoupledlstmcell_kernel(tc, x, h, c, q, w_bytes, w_scal
         differ(6)
         finish(4)
         finish(5)
-        product(7)
-        lo, hi = slice(0, BANK // 2), slice(BANK // 2, BANK)
-        add_up(7, 1)
-        add_up(7, 0, lo)
-        add_up(7, 0, hi)
         weigh(6)
-        differ(7)
+        lo, hi = slice(0, BANK // 2), slice(BANK // 2, BANK)
+        product(7, 1)
+        product(7, 0, lo)
+        product(7, 0, hi)
+        add_up(7, 1)
         finish(6)
+        add_up(7, 0, lo)
+        differ(7)
+        add_up(7, 0, hi)
         weigh(7, lo)
         weigh(7, hi)
         finish(7, lo)

@@ -23,6 +23,7 @@ PASSES = D // (P * PACK)
 KC = H // P
 BANK = 512
 SCALAR_TILES = (7,)
+VECTOR_TILES = (0, 1, 2, 3)
 
 FLOPS = 2 * N * H * D + 2 * N * H * G + 2 * N * D * G
 
@@ -54,9 +55,13 @@ def tile_mogrifieroneroundcoupledlstmcell_kernel(tc, x, h, c, q, w_bytes, w_scal
         nc.vector.memset(brow[:], 0.0)
         ones = keep.tile([P, P], BF16, name="ones")
         nc.vector.memset(ones[:], 1.0)
-        for k in range(4):
+
+        def keep_clock(times):
             bank = ring.tile([P, BANK], F32, name="bank_7")
-            nc.tensor.matmul(bank[:], lhsT=idle[:, 0:P], rhs=idle[:], start=True, stop=True)
+            for k in range(times):
+                nc.tensor.matmul(bank[:], lhsT=idle[:, 0:P], rhs=idle[:], start=True, stop=True)
+
+        keep_clock(4)
 
         hv = h.rearrange("(s p j) k -> s p j k", s=HALVES, p=P)
         xv = x.rearrange("(s p j) k -> s p j k", s=HALVES, p=P)
@@ -86,8 +91,8 @@ def tile_mogrifieroneroundcoupledlstmcell_kernel(tc, x, h, c, q, w_bytes, w_scal
         w_sc = keep.tile([P, PASSES, PACK], F32, name="w_sc")
 
         nc.scalar.activation(out=scratch[:], in_=scratch[:], func=ACT.Sigmoid)
-        for j in range(0, TILES, 2):
-            nc.sync.dma_start(out=h_sb[0][:, j : j + 2, :], in_=hv[0][:, j : j + 2, :])
+        for j in range(TILES):
+            nc.sync.dma_start(out=h_sb[0][:, j, :], in_=hv[0][:, j, :])
         nc.sync.dma_start(out=q_sb[0][:], in_=qv[:, :, 0:BANK])
         nc.sync.dma_start(out=w_sc[:], in_=sv)
         nc.sync.dma_start(out=w_by[0][:], in_=wv[0])
@@ -106,8 +111,6 @@ def tile_mogrifieroneroundcoupledlstmcell_kernel(tc, x, h, c, q, w_bytes, w_scal
             hT_half = keep.tile([P, TILES, KC, P], BF16, name=f"hT{s}")
             hT.append(hT_half)
             for g in range(PASSES):
-                sig_t = keep.tile([P, PACK, HALF], F32, name=f"sig{s}{g}")
-                sig[s, g] = sig_t
                 xw_t = keep.tile([P, TILES, 2, P], F32, name=f"xw{s}{g}")
                 xw[s, g] = xw_t
                 x1_t = keep.tile([P, HALF, PACK], BF16, name=f"x1_{s}{g}", align_bytes=64)
@@ -126,7 +129,7 @@ def tile_mogrifieroneroundcoupledlstmcell_kernel(tc, x, h, c, q, w_bytes, w_scal
             wq.append(wq_t)
             ws_t = keep.tile([P, G], U8, name=f"ws{g}", align_bytes=64)
             ws.append(ws_t)
-        bias = keep.tile([P, BANK], F32, name="bias")
+        bias = keep.tile([P, G], F32, name="bias")
 
         def turn_h(i, engine):
             s, j = divmod(i, TILES)
@@ -136,6 +139,9 @@ def tile_mogrifieroneroundcoupledlstmcell_kernel(tc, x, h, c, q, w_bytes, w_scal
             engine(out=hT[s][:, j, :, :], in_=bank[:])
 
         def gate_logits(s, g, t):
+            if t == 0:
+                sig_t = work.tile([P, PACK, HALF], F32, name=turn("sig", 3))
+                sig[s, g] = sig_t
             bank = ring.tile([P, BANK], F32, name=turn("bank", 8))
             for kc in range(KC):
                 nc.tensor.matmul(
@@ -147,9 +153,9 @@ def tile_mogrifieroneroundcoupledlstmcell_kernel(tc, x, h, c, q, w_bytes, w_scal
                 )
             nc.scalar.activation(out=sig[s, g][:, t, :], in_=bank[:], func=ACT.Sigmoid)
 
-        def order_x(s, g):
+        def order_x(s, g, engine):
             words = x_sb[s][:].bitcast(F32).rearrange("p j (g m u) -> p j g u m", g=PASSES, u=2)
-            nc.scalar.copy(out=xw[s, g][:], in_=words[:, :, g, :, :])
+            engine(out=xw[s, g][:], in_=words[:, :, g, :, :])
 
         xbank = {}
 
@@ -179,26 +185,17 @@ def tile_mogrifieroneroundcoupledlstmcell_kernel(tc, x, h, c, q, w_bytes, w_scal
                 in_=x1[s, g][:].rearrange("p n t -> p (n t)"),
             )
 
-        def widen_v(g, t):
-            nc.vector.tensor_scalar(
-                out=wide[g][:, t, :],
-                in0=w_by[g][:, t, :].bitcast(FP8),
-                scalar1=w_sc[:, g, t : t + 1],
-                scalar2=None,
-                op0=ALU.mult,
-            )
+        def widen(g, t, on_scalar=False):
+            codes = w_by[g][:, t, :].bitcast(FP8)
+            scale = w_sc[:, g, t : t + 1]
+            if on_scalar:
+                nc.scalar.activation(out=wide[g][:, t, :], in_=codes, func=ACT.Copy, scale=scale)
+            else:
+                nc.vector.tensor_scalar(out=wide[g][:, t, :], in0=codes, scalar1=scale, scalar2=None, op0=ALU.mult)
 
-        def widen_s(g, t):
-            nc.scalar.activation(
-                out=wide[g][:, t, :],
-                in_=w_by[g][:, t, :].bitcast(FP8),
-                func=ACT.Copy,
-                scale=w_sc[:, g, t : t + 1],
-            )
-
-        def interleave_w(g, j):
+        def interleave_w(g, j, engine):
             n = slice(j * BANK, (j + 1) * BANK)
-            nc.vector.tensor_copy(out=wi[g][:, n, :], in_=wide[g][:, :, n].rearrange("p t n -> p n t"))
+            engine(out=wi[g][:, n, :], in_=wide[g][:, :, n].rearrange("p t n -> p n t"))
 
         def quantize_w(g, j):
             n = slice(j * BANK, (j + 1) * BANK)
@@ -208,18 +205,21 @@ def tile_mogrifieroneroundcoupledlstmcell_kernel(tc, x, h, c, q, w_bytes, w_scal
                 in_=wi[g][:, n, :].rearrange("p n t -> p (n t)"),
             )
 
-        def spread_bias():
+        def spread_bias(k):
             bank = ring.tile([P, BANK], F32, name=turn("bank", 8))
-            nc.tensor.matmul(bank[:], lhsT=ones[:], rhs=brow[:, BANK:G], start=True, stop=True)
-            nc.scalar.copy(out=bias[:], in_=bank[:])
+            nc.tensor.matmul(bank[:], lhsT=ones[:], rhs=brow[:, k * BANK : (k + 1) * BANK], start=True, stop=True)
+            nc.scalar.copy(out=bias[:, k * BANK : (k + 1) * BANK], in_=bank[:])
 
         hub, hubank = {}, {}
+
+        def on_vector(i, k):
+            return i in VECTOR_TILES or (k == 1 and i not in SCALAR_TILES)
 
         def hidden(i):
             s, j = divmod(i, TILES)
             for k in (1, 0):
                 bank = ring.tile([P, BANK], F32, name=turn("bank", 8))
-                biased = k == 0 or i in SCALAR_TILES
+                biased = not on_vector(i, k)
                 if biased:
                     nc.tensor.matmul(
                         bank[:], lhsT=ones[:], rhs=brow[:, k * BANK : (k + 1) * BANK], start=True, stop=False
@@ -235,10 +235,12 @@ def tile_mogrifieroneroundcoupledlstmcell_kernel(tc, x, h, c, q, w_bytes, w_scal
                 hubank[i, k] = bank
 
         def keep_hidden(i, k):
-            hub_t = work.tile([P, BANK], F32, name=turn(f"hub{k}", 4))
+            hub_t = work.tile([P, BANK], F32, name=turn(f"hub{k}", 6))
             hub[i, k] = hub_t
-            if k == 1 and i not in SCALAR_TILES:
-                nc.vector.tensor_tensor(out=hub_t[:], in0=hubank[i, k][:], in1=bias[:], op=ALU.add)
+            if on_vector(i, k):
+                nc.vector.tensor_tensor(
+                    out=hub_t[:], in0=hubank[i, k][:], in1=bias[:, k * BANK : (k + 1) * BANK], op=ALU.add
+                )
             else:
                 nc.scalar.copy(out=hub_t[:], in_=hubank[i, k][:])
 
@@ -283,9 +285,9 @@ def tile_mogrifieroneroundcoupledlstmcell_kernel(tc, x, h, c, q, w_bytes, w_scal
         def weigh(i, n=slice(0, BANK)):
             nc.vector.tensor_tensor(out=low[i][:, n], in0=low[i][:, n], in1=act[i, 0][:, n], op=ALU.mult)
 
-        def finish(i, n=slice(0, BANK)):
+        def finish(i, n=slice(0, BANK), engine=nc.gpsimd):
             s, j = divmod(i, TILES)
-            nc.vector.tensor_tensor(out=low[i][:, n], in0=low[i][:, n], in1=c_sb[s][:, j, n], op=ALU.add)
+            engine.tensor_tensor(out=low[i][:, n], in0=low[i][:, n], in1=c_sb[s][:, j, n], op=ALU.add)
             nc.sync.dma_start(out=ov[s][:, j, n], in_=low[i][:, n])
 
         vcopy, scopy = nc.vector.tensor_copy, nc.scalar.copy
@@ -294,124 +296,126 @@ def tile_mogrifieroneroundcoupledlstmcell_kernel(tc, x, h, c, q, w_bytes, w_scal
             for j in range(TILES):
                 turn_h(s * TILES + j, vcopy if j % 2 == 0 else scopy)
 
-        turn_half(0)
-        for t in range(PACK):
-            widen_v(0, t)
-        for t in range(PACK):
-            gate_logits(0, 0, t)
-            if t == 1:
-                order_x(0, 0)
-        for j in range(2):
-            interleave_w(0, j)
-        for j in range(2):
-            quantize_w(0, j)
-        order_x(0, 1)
-        for t in range(PACK):
-            gate_logits(0, 1, t)
-            if t == 1:
-                widen_s(1, 2)
-        widen_s(1, 3)
-        spread_bias()
-        turn_x(0, 0)
-        widen_v(1, 0)
-        widen_v(1, 1)
-        gate_x(0, 0, 0)
-        turn_half(1)
-        turn_x(0, 1)
-        order_x(1, 0)
-        order_x(1, 1)
-        gate_x(0, 0, 1)
-        gate_x(0, 1, 0)
-        gate_x(0, 1, 1)
-        for t in range(PACK):
-            gate_logits(1, 0, t)
-        interleave_w(1, 0)
-        interleave_w(1, 1)
-        quantize_x(0, 0)
-        quantize_x(0, 1)
-        quantize_w(1, 1)
-        quantize_w(1, 0)
+        def keep_both(i):
+            keep_hidden(i, 1)
+            keep_hidden(i, 0)
 
-        def keep_pair(i):
-            for m in (i, i + 1):
-                keep_hidden(m, 1)
-                keep_hidden(m, 0)
+        def product_both(i):
+            product(i, 1)
+            product(i, 0)
 
-        hidden(0)
-        hidden(1)
-        keep_pair(0)
-        product(0, 1)
-        product(0, 0)
-        product(1, 1)
-        product(1, 0)
-        turn_x(1, 0)
-        for i in (0, 1):
+        def add_both(i):
             add_up(i, 1)
             add_up(i, 0)
+
+        lo, hi = slice(0, BANK // 2), slice(BANK // 2, BANK)
+
+        turn_half(0)
+        keep_clock(1)
+        for t in range(PACK):
+            widen(0, t)
+        for t in range(PACK):
+            gate_logits(0, 0, t)
+        interleave_w(0, 1, vcopy)
+        order_x(0, 0, vcopy)
+        order_x(0, 1, vcopy)
+        interleave_w(0, 0, vcopy)
+        quantize_w(0, 1)
+        for t in range(PACK):
+            gate_logits(0, 1, t)
+        for t in range(PACK):
+            widen(1, t)
+        quantize_w(0, 0)
+        spread_bias(1)
+        spread_bias(0)
+        turn_x(0, 0)
+        interleave_w(1, 1, scopy)
+        gate_x(0, 0, 0)
+        gate_x(0, 0, 1)
+        turn_half(1)
+        turn_x(0, 1)
+        interleave_w(1, 0, scopy)
+        gate_x(0, 1, 0)
+        gate_x(0, 1, 1)
+        hidden(0)
+        quantize_w(1, 1)
+        quantize_x(0, 0)
+        quantize_x(0, 1)
+        keep_hidden(0, 1)
+        for t in range(PACK):
+            gate_logits(1, 0, t)
+            if t == 1:
+                order_x(1, 0, scopy)
+        quantize_w(1, 0)
+        keep_hidden(0, 0)
+        order_x(1, 1, scopy)
+        hidden(1)
+        keep_both(1)
+        product_both(0)
+        product_both(1)
+        turn_x(1, 0)
+        add_both(0)
+        add_both(1)
         gate_x(1, 0, 0)
         gate_x(1, 0, 1)
-        differ(0)
+        hidden(2)
+        keep_both(2)
         quantize_x(1, 0)
-        differ(1)
         for t in range(PACK):
             gate_logits(1, 1, t)
         turn_x(1, 1)
+        differ(0)
+        differ(1)
         weigh(0)
         weigh(1)
-        finish(0)
         gate_x(1, 1, 0)
+        finish(0)
         gate_x(1, 1, 1)
-        hidden(2)
-        keep_hidden(2, 1)
-        keep_hidden(2, 0)
-        quantize_x(1, 1)
         finish(1)
         hidden(3)
-        keep_hidden(3, 1)
-        keep_hidden(3, 0)
-        for i in (2, 4):
-            product(i, 1)
-            product(i, 0)
-            product(i + 1, 1)
-            product(i + 1, 0)
-            for m in (i, i + 1):
-                add_up(m, 1)
-                add_up(m, 0)
-            hidden(i + 2)
-            differ(i)
-            keep_hidden(i + 2, 1)
-            keep_hidden(i + 2, 0)
-            differ(i + 1)
-            weigh(i)
-            if i == 2:
-                weigh(i + 1)
-                hidden(i + 3)
-                keep_hidden(i + 3, 1)
-                keep_hidden(i + 3, 0)
-                finish(i)
-                finish(i + 1)
-        product(6, 1)
-        product(6, 0)
-        add_up(6, 1)
-        add_up(6, 0)
+        keep_both(3)
+        quantize_x(1, 1)
+        product_both(2)
+        product_both(3)
+        add_both(2)
+        add_both(3)
+        hidden(4)
+        keep_both(4)
+        differ(2)
+        differ(3)
+        hidden(5)
+        keep_both(5)
+        weigh(2)
+        weigh(3)
+        product_both(4)
+        product_both(5)
+        add_both(4)
+        finish(2)
+        add_both(5)
+        finish(3)
+        differ(4)
+        hidden(6)
+        keep_both(6)
+        differ(5)
+        weigh(4)
+        product_both(6)
+        add_both(6)
+        finish(4)
         weigh(5)
         hidden(7)
-        keep_hidden(7, 1)
-        keep_hidden(7, 0)
-        differ(6)
-        finish(4)
+        keep_both(7)
         finish(5)
+        differ(6)
         weigh(6)
-        lo, hi = slice(0, BANK // 2), slice(BANK // 2, BANK)
         product(7, 1)
         product(7, 0, lo)
         product(7, 0, hi)
         add_up(7, 1)
         finish(6)
         add_up(7, 0, lo)
-        differ(7)
         add_up(7, 0, hi)
+        differ(7)
         weigh(7, lo)
         weigh(7, hi)
-        finish(7, lo)
-        finish(7, hi)
+        finish(7, lo, engine=nc.vector)
+        finish(7, hi, engine=nc.vector)

@@ -22,7 +22,7 @@ TILES = HALF // P
 PASSES = D // (P * PACK)
 KC = H // P
 BANK = 512
-SCALAR_TILES = (7,)
+SCALAR_TILES = (6, 7)
 VECTOR_TILES = (0, 1, 2, 3)
 
 FLOPS = 2 * N * H * D + 2 * N * H * G + 2 * N * D * G
@@ -61,7 +61,7 @@ def tile_mogrifieroneroundcoupledlstmcell_kernel(tc, x, h, c, q, w_bytes, w_scal
             for k in range(times):
                 nc.tensor.matmul(bank[:], lhsT=idle[:, 0:P], rhs=idle[:], start=True, stop=True)
 
-        keep_clock(4)
+        keep_clock(5)
 
         hv = h.rearrange("(s p j) k -> s p j k", s=HALVES, p=P)
         xv = x.rearrange("(s p j) k -> s p j k", s=HALVES, p=P)
@@ -91,18 +91,19 @@ def tile_mogrifieroneroundcoupledlstmcell_kernel(tc, x, h, c, q, w_bytes, w_scal
         w_sc = keep.tile([P, PASSES, PACK], F32, name="w_sc")
 
         nc.scalar.activation(out=scratch[:], in_=scratch[:], func=ACT.Sigmoid)
-        for j in range(TILES):
-            nc.sync.dma_start(out=h_sb[0][:, j, :], in_=hv[0][:, j, :])
-        nc.sync.dma_start(out=q_sb[0][:], in_=qv[:, :, 0:BANK])
+        for j in range(0, TILES, 2):
+            nc.sync.dma_start(out=h_sb[0][:, j : j + 2, :], in_=hv[0][:, j : j + 2, :])
+        for kc in range(KC):
+            nc.sync.dma_start(out=q_sb[0][:, kc, :], in_=qv[:, kc, 0:BANK])
         nc.sync.dma_start(out=w_sc[:], in_=sv)
         nc.sync.dma_start(out=w_by[0][:], in_=wv[0])
         nc.sync.dma_start(out=brow[0:1, :], in_=b.rearrange("(o n) -> o n", o=1))
-        nc.sync.dma_start(out=x_sb[0][:], in_=xv[0])
         nc.sync.dma_start(out=q_sb[1][:], in_=qv[:, :, BANK:D])
         nc.sync.dma_start(out=h_sb[1][:], in_=hv[1])
+        nc.sync.dma_start(out=x_sb[0][:], in_=xv[0])
         nc.sync.dma_start(out=w_by[1][:], in_=wv[1])
-        nc.sync.dma_start(out=x_sb[1][:], in_=xv[1])
         nc.sync.dma_start(out=u_sb[:], in_=uv)
+        nc.sync.dma_start(out=x_sb[1][:], in_=xv[1])
         for s in range(HALVES):
             nc.sync.dma_start(out=c_sb[s][:], in_=cv[s])
 
@@ -138,20 +139,25 @@ def tile_mogrifieroneroundcoupledlstmcell_kernel(tc, x, h, c, q, w_bytes, w_scal
                 nc.tensor.transpose(bank[:, kc, :], h_sb[s][:, j, kc * P : (kc + 1) * P], ident16[:])
             engine(out=hT[s][:, j, :, :], in_=bank[:])
 
-        def gate_logits(s, g, t):
-            if t == 0:
+        def gate_logits(s, g, *planes):
+            if planes[0] == 0:
                 sig_t = work.tile([P, PACK, HALF], F32, name=turn("sig", 3))
                 sig[s, g] = sig_t
-            bank = ring.tile([P, BANK], F32, name=turn("bank", 8))
+            banks = {}
+            for t in planes:
+                bank = ring.tile([P, BANK], F32, name=turn("bank", 8))
+                banks[t] = bank
             for kc in range(KC):
-                nc.tensor.matmul(
-                    bank[:],
-                    lhsT=q_sb[g][:, kc, t:BANK:PACK],
-                    rhs=hT[s][:, :, kc, :],
-                    start=(kc == 0),
-                    stop=(kc == KC - 1),
-                )
-            nc.scalar.activation(out=sig[s, g][:, t, :], in_=bank[:], func=ACT.Sigmoid)
+                for t in planes:
+                    nc.tensor.matmul(
+                        banks[t][:],
+                        lhsT=q_sb[g][:, kc, t:BANK:PACK],
+                        rhs=hT[s][:, :, kc, :],
+                        start=(kc == 0),
+                        stop=(kc == KC - 1),
+                    )
+            for t in planes:
+                nc.scalar.activation(out=sig[s, g][:, t, :], in_=banks[t][:], func=ACT.Sigmoid)
 
         def order_x(s, g, engine):
             words = x_sb[s][:].bitcast(F32).rearrange("p j (g m u) -> p j g u m", g=PASSES, u=2)
@@ -215,9 +221,9 @@ def tile_mogrifieroneroundcoupledlstmcell_kernel(tc, x, h, c, q, w_bytes, w_scal
         def on_vector(i, k):
             return i in VECTOR_TILES or (k == 1 and i not in SCALAR_TILES)
 
-        def hidden(i):
+        def hidden(i, ks=(1, 0)):
             s, j = divmod(i, TILES)
-            for k in (1, 0):
+            for k in ks:
                 bank = ring.tile([P, BANK], F32, name=turn("bank", 8))
                 biased = not on_vector(i, k)
                 if biased:
@@ -295,6 +301,8 @@ def tile_mogrifieroneroundcoupledlstmcell_kernel(tc, x, h, c, q, w_bytes, w_scal
         def turn_half(s):
             for j in range(TILES):
                 turn_h(s * TILES + j, vcopy if j % 2 == 0 else scopy)
+                if s == 0 and j == TILES - 1:
+                    keep_clock(1)
 
         def keep_both(i):
             keep_hidden(i, 1)
@@ -311,43 +319,44 @@ def tile_mogrifieroneroundcoupledlstmcell_kernel(tc, x, h, c, q, w_bytes, w_scal
         lo, hi = slice(0, BANK // 2), slice(BANK // 2, BANK)
 
         turn_half(0)
-        keep_clock(1)
         for t in range(PACK):
             widen(0, t)
-        for t in range(PACK):
-            gate_logits(0, 0, t)
+        gate_logits(0, 0, 0, 1)
+        gate_logits(0, 0, 2, 3)
         interleave_w(0, 1, vcopy)
-        order_x(0, 0, vcopy)
-        order_x(0, 1, vcopy)
+        gate_logits(0, 1, 0)
+        gate_logits(0, 1, 1)
         interleave_w(0, 0, vcopy)
+        turn_half(1)
         quantize_w(0, 1)
-        for t in range(PACK):
-            gate_logits(0, 1, t)
+        quantize_w(0, 0)
+        order_x(0, 0, scopy)
+        gate_logits(0, 1, 2)
+        order_x(0, 1, scopy)
+        gate_logits(0, 1, 3)
         for t in range(PACK):
             widen(1, t)
-        quantize_w(0, 0)
+        turn_x(0, 0)
         spread_bias(1)
         spread_bias(0)
-        turn_x(0, 0)
-        interleave_w(1, 1, scopy)
         gate_x(0, 0, 0)
         gate_x(0, 0, 1)
-        turn_half(1)
+        interleave_w(1, 1, scopy)
         turn_x(0, 1)
         interleave_w(1, 0, scopy)
         gate_x(0, 1, 0)
         gate_x(0, 1, 1)
-        hidden(0)
         quantize_w(1, 1)
         quantize_x(0, 0)
         quantize_x(0, 1)
-        keep_hidden(0, 1)
-        for t in range(PACK):
-            gate_logits(1, 0, t)
-            if t == 1:
-                order_x(1, 0, scopy)
+        gate_logits(1, 0, 0)
+        gate_logits(1, 0, 1)
+        hidden(0)
         quantize_w(1, 0)
-        keep_hidden(0, 0)
+        keep_both(0)
+        gate_logits(1, 0, 2)
+        order_x(1, 0, scopy)
+        gate_logits(1, 0, 3)
         order_x(1, 1, scopy)
         hidden(1)
         keep_both(1)
@@ -393,28 +402,30 @@ def tile_mogrifieroneroundcoupledlstmcell_kernel(tc, x, h, c, q, w_bytes, w_scal
         finish(2)
         add_both(5)
         finish(3)
-        differ(4)
         hidden(6)
         keep_both(6)
+        differ(4)
         differ(5)
-        weigh(4)
         product_both(6)
+        weigh(4)
+        weigh(5)
         add_both(6)
         finish(4)
-        weigh(5)
-        hidden(7)
-        keep_both(7)
-        finish(5)
-        differ(6)
-        weigh(6)
+        hidden(7, (1,))
+        keep_hidden(7, 1)
         product(7, 1)
+        finish(5, engine=nc.vector)
+        differ(6)
+        hidden(7, (0,))
+        weigh(6)
+        add_up(7, 1)
+        keep_hidden(7, 0)
+        finish(6, engine=nc.vector)
+        differ(7)
         product(7, 0, lo)
         product(7, 0, hi)
-        add_up(7, 1)
-        finish(6)
         add_up(7, 0, lo)
         add_up(7, 0, hi)
-        differ(7)
         weigh(7, lo)
         weigh(7, hi)
         finish(7, lo, engine=nc.vector)

from contextlib import ExitStack

import concourse.mybir as mybir
from concourse.masks import make_identity

F32 = mybir.dt.float32
BF16 = mybir.dt.bfloat16
U32 = mybir.dt.uint32
U8 = mybir.dt.uint8
FP8 = mybir.dt.float8_e4m3fn
FP8X4 = mybir.dt.float8_e4m3fn_x4
ACT = mybir.ActivationFunctionType
ALU = mybir.AluOpType

N, D, H = 1024, 1024, 512
G = 2 * H
P = 128
PACK = 4
HALVES = 2
HALF = N // HALVES
TILES = HALF // P
PASSES = D // (P * PACK)
KC = H // P
BANK = 512
SCALAR_TILES = (6, 7)
VECTOR_TILES = (0, 1, 2, 3)

FLOPS = 2 * N * H * D + 2 * N * H * G + 2 * N * D * G


def tile_mogrifieroneroundcoupledlstmcell_kernel(tc, x, h, c, q, w_bytes, w_scale, u, b, out):
    nc = tc.nc
    with ExitStack() as ctx:
        keep = ctx.enter_context(tc.tile_pool(name="keep", bufs=1))
        work = ctx.enter_context(tc.tile_pool(name="work", bufs=1))
        ring = ctx.enter_context(tc.psum_pool(name="ring", bufs=1))
        counts = {}

        def turn(name, length):
            counts[name] = counts.get(name, -1) + 1
            return f"{name}_{counts[name] % length}"

        ident16 = keep.tile([P, P], BF16, name="ident16")
        make_identity(nc, ident16[:])
        ident32 = keep.tile([P, P], F32, name="ident32")
        make_identity(nc, ident32[:])

        ctx.enter_context(tc.manual_schedule())

        idle = keep.tile([P, BANK], BF16, name="idle")
        nc.vector.memset(idle[:], 0.0)
        scratch = keep.tile([P, 1], F32, name="scratch")
        nc.vector.memset(scratch[:], 0.0)
        brow = keep.tile([P, G], BF16, name="brow")
        nc.vector.memset(brow[:], 0.0)
        ones = keep.tile([P, P], BF16, name="ones")
        nc.vector.memset(ones[:], 1.0)

        def keep_clock(times):
            bank = ring.tile([P, BANK], F32, name="bank_7")
            for k in range(times):
                nc.tensor.matmul(bank[:], lhsT=idle[:, 0:P], rhs=idle[:], start=True, stop=True)

        keep_clock(5)

        hv = h.rearrange("(s p j) k -> s p j k", s=HALVES, p=P)
        xv = x.rearrange("(s p j) k -> s p j k", s=HALVES, p=P)
        cv = c.rearrange("(s p j) k -> s p j k", s=HALVES, p=P)
        ov = out.rearrange("(s p j) k -> s p j k", s=HALVES, p=P)
        qv = q.rearrange("(kc p) d -> p kc d", p=P)
        uv = u.rearrange("(kc p) n -> p kc n", p=P)
        wv = w_bytes.rearrange("(g p t) n -> g p t n", p=P, t=PACK)
        sv = w_scale.rearrange("(g p t) o -> p g (t o)", p=P, t=PACK)

        h_sb, x_sb, c_sb, w_by = [], [], [], []
        for s in range(HALVES):
            h_half = keep.tile([P, TILES, H], BF16, name=f"h{s}")
            h_sb.append(h_half)
            x_half = keep.tile([P, TILES, D], BF16, name=f"x{s}")
            x_sb.append(x_half)
            c_half = keep.tile([P, TILES, H], BF16, name=f"c{s}")
            c_sb.append(c_half)
        for g in range(PASSES):
            w_half = keep.tile([P, PACK, G], U8, name=f"wb{g}")
            w_by.append(w_half)
        q_sb = []
        for g in range(PASSES):
            q_half = keep.tile([P, KC, BANK], BF16, name=f"q{g}")
            q_sb.append(q_half)
        u_sb = keep.tile([P, KC, G], BF16, name="u_sb")
        w_sc = keep.tile([P, PASSES, PACK], F32, name="w_sc")

        nc.scalar.activation(out=scratch[:], in_=scratch[:], func=ACT.Sigmoid)
        for j in range(0, TILES, 2):
            nc.sync.dma_start(out=h_sb[0][:, j : j + 2, :], in_=hv[0][:, j : j + 2, :])
        for kc in range(KC):
            nc.sync.dma_start(out=q_sb[0][:, kc, :], in_=qv[:, kc, 0:BANK])
        nc.sync.dma_start(out=w_sc[:], in_=sv)
        nc.sync.dma_start(out=w_by[0][:], in_=wv[0])
        nc.sync.dma_start(out=brow[0:1, :], in_=b.rearrange("(o n) -> o n", o=1))
        nc.sync.dma_start(out=q_sb[1][:], in_=qv[:, :, BANK:D])
        nc.sync.dma_start(out=h_sb[1][:], in_=hv[1])
        nc.sync.dma_start(out=x_sb[0][:], in_=xv[0])
        nc.sync.dma_start(out=w_by[1][:], in_=wv[1])
        nc.sync.dma_start(out=u_sb[:], in_=uv)
        nc.sync.dma_start(out=x_sb[1][:], in_=xv[1])
        for s in range(HALVES):
            nc.sync.dma_start(out=c_sb[s][:], in_=cv[s])

        hT, xw, sig, x1, xq, xs = [], {}, {}, {}, {}, {}
        for s in range(HALVES):
            hT_half = keep.tile([P, TILES, KC, P], BF16, name=f"hT{s}")
            hT.append(hT_half)
            for g in range(PASSES):
                xw_t = keep.tile([P, TILES, 2, P], F32, name=f"xw{s}{g}")
                xw[s, g] = xw_t
                x1_t = keep.tile([P, HALF, PACK], BF16, name=f"x1_{s}{g}", align_bytes=64)
                x1[s, g] = x1_t
                xq_t = keep.tile([P, HALF], U32, name=f"xq{s}{g}", align_bytes=64)
                xq[s, g] = xq_t
                xs_t = keep.tile([P, HALF], U8, name=f"xs{s}{g}", align_bytes=64)
                xs[s, g] = xs_t
        wide, wi, wq, ws = [], [], [], []
        for g in range(PASSES):
            wide_t = keep.tile([P, PACK, G], BF16, name=f"wide{g}")
            wide.append(wide_t)
            wi_t = keep.tile([P, G, PACK], BF16, name=f"wi{g}", align_bytes=64)
            wi.append(wi_t)
            wq_t = keep.tile([P, G], U32, name=f"wq{g}", align_bytes=64)
            wq.append(wq_t)
            ws_t = keep.tile([P, G], U8, name=f"ws{g}", align_bytes=64)
            ws.append(ws_t)
        bias = keep.tile([P, G], F32, name="bias")

        def turn_h(i, engine):
            s, j = divmod(i, TILES)
            bank = ring.tile([P, KC, P], BF16, name=turn("bank", 8))
            for kc in range(KC):
                nc.tensor.transpose(bank[:, kc, :], h_sb[s][:, j, kc * P : (kc + 1) * P], ident16[:])
            engine(out=hT[s][:, j, :, :], in_=bank[:])

        def gate_logits(s, g, *planes):
            if planes[0] == 0:
                sig_t = work.tile([P, PACK, HALF], F32, name=turn("sig", 3))
                sig[s, g] = sig_t
            banks = {}
            for t in planes:
                bank = ring.tile([P, BANK], F32, name=turn("bank", 8))
                banks[t] = bank
            for kc in range(KC):
                for t in planes:
                    nc.tensor.matmul(
                        banks[t][:],
                        lhsT=q_sb[g][:, kc, t:BANK:PACK],
                        rhs=hT[s][:, :, kc, :],
                        start=(kc == 0),
                        stop=(kc == KC - 1),
                    )
            for t in planes:
                nc.scalar.activation(out=sig[s, g][:, t, :], in_=banks[t][:], func=ACT.Sigmoid)

        def order_x(s, g, engine):
            words = x_sb[s][:].bitcast(F32).rearrange("p j (g m u) -> p j g u m", g=PASSES, u=2)
            engine(out=xw[s, g][:], in_=words[:, :, g, :, :])

        xbank = {}

        def turn_x(s, g):
            for pr in range(2):
                bank = ring.tile([P, 2, 2 * P], F32, name=turn("bank", 8))
                for jj in range(2):
                    for v in range(2):
                        nc.tensor.transpose(
                            bank[:, v, jj * P : (jj + 1) * P], xw[s, g][:, 2 * pr + jj, v, :], ident32[:]
                        )
                xbank[s, g, pr] = bank

        def gate_x(s, g, pr):
            n = slice(pr * 2 * P, (pr + 1) * 2 * P)
            nc.vector.tensor_tensor(
                out=x1[s, g][:, n, :].rearrange("p n (u e) -> p n u e", u=2),
                in0=sig[s, g][:, :, n].rearrange("p (u e) n -> p n u e", u=2),
                in1=xbank[s, g, pr][:].bitcast(BF16).rearrange("p u (n e) -> p n u e", e=2),
                op=ALU.mult,
            )

        def quantize_x(s, g):
            nc.vector.quantize_mx(
                out=xq[s, g][:].bitcast(FP8X4),
                scales=xs[s, g][:],
                in_=x1[s, g][:].rearrange("p n t -> p (n t)"),
            )

        def widen(g, t, on_scalar=False):
            codes = w_by[g][:, t, :].bitcast(FP8)
            scale = w_sc[:, g, t : t + 1]
            if on_scalar:
                nc.scalar.activation(out=wide[g][:, t, :], in_=codes, func=ACT.Copy, scale=scale)
            else:
                nc.vector.tensor_scalar(out=wide[g][:, t, :], in0=codes, scalar1=scale, scalar2=None, op0=ALU.mult)

        def interleave_w(g, j, engine):
            n = slice(j * BANK, (j + 1) * BANK)
            engine(out=wi[g][:, n, :], in_=wide[g][:, :, n].rearrange("p t n -> p n t"))

        def quantize_w(g, j):
            n = slice(j * BANK, (j + 1) * BANK)
            nc.vector.quantize_mx(
                out=wq[g][:, n].bitcast(FP8X4),
                scales=ws[g][:, n],
                in_=wi[g][:, n, :].rearrange("p n t -> p (n t)"),
            )

        def spread_bias(k):
            bank = ring.tile([P, BANK], F32, name=turn("bank", 8))
            nc.tensor.matmul(bank[:], lhsT=ones[:], rhs=brow[:, k * BANK : (k + 1) * BANK], start=True, stop=True)
            nc.scalar.copy(out=bias[:, k * BANK : (k + 1) * BANK], in_=bank[:])

        hub, hubank = {}, {}

        def on_vector(i, k):
            return i in VECTOR_TILES or (k == 1 and i not in SCALAR_TILES)

        def hidden(i, ks=(1, 0)):
            s, j = divmod(i, TILES)
            for k in ks:
                bank = ring.tile([P, BANK], F32, name=turn("bank", 8))
                biased = not on_vector(i, k)
                if biased:
                    nc.tensor.matmul(
                        bank[:], lhsT=ones[:], rhs=brow[:, k * BANK : (k + 1) * BANK], start=True, stop=False
                    )
                for kc in range(KC):
                    nc.tensor.matmul(
                        bank[:],
                        lhsT=hT[s][:, j, kc, :],
                        rhs=u_sb[:, kc, k * BANK : (k + 1) * BANK],
                        start=(kc == 0 and not biased),
                        stop=(kc == KC - 1),
                    )
                hubank[i, k] = bank

        def keep_hidden(i, k):
            hub_t = work.tile([P, BANK], F32, name=turn(f"hub{k}", 6))
            hub[i, k] = hub_t
            if on_vector(i, k):
                nc.vector.tensor_tensor(
                    out=hub_t[:], in0=hubank[i, k][:], in1=bias[:, k * BANK : (k + 1) * BANK], op=ALU.add
                )
            else:
                nc.scalar.copy(out=hub_t[:], in_=hubank[i, k][:])

        mxbank = {}

        def product(i, k, n=slice(0, BANK)):
            s, j = divmod(i, TILES)
            cols = slice(k * BANK + n.start, k * BANK + n.stop)
            bank = ring.tile([P, n.stop - n.start], F32, name=turn("bank", 8))
            for g in range(PASSES):
                nc.tensor.matmul_mx(
                    out=bank[:],
                    lhsT=xq[s, g][:, j * P : (j + 1) * P].bitcast(FP8X4),
                    lhsT_scale=xs[s, g][:, j * P : (j + 1) * P],
                    rhs=wq[g][:, cols].bitcast(FP8X4),
                    rhs_scale=ws[g][:, cols],
                    start=(g == 0),
                    stop=(g == PASSES - 1),
                )
            mxbank[i, k, n.start] = bank

        pre, act, low = {}, {}, {}

        def add_up(i, k, n=slice(0, BANK)):
            if (i, k) not in pre:
                pre_t = work.tile([P, BANK], F32, name=turn(f"pre{k}", 4))
                pre[i, k] = pre_t
                act[i, k] = pre_t
            nc.vector.scalar_tensor_tensor(
                out=pre[i, k][:, n], in0=mxbank[i, k, n.start][:], scalar=2.0, in1=hub[i, k][:, n], op0=ALU.mult, op1=ALU.add
            )
            nc.scalar.activation(
                out=act[i, k][:, n], in_=pre[i, k][:, n], func=(ACT.Tanh if k else ACT.Sigmoid)
            )

        def differ(i):
            s, j = divmod(i, TILES)
            low_t = work.tile([P, BANK], F32, name=turn("low", 4))
            low[i] = low_t
            nc.vector.tensor_tensor(out=low_t[:], in0=act[i, 1][:], in1=c_sb[s][:, j, :], op=ALU.subtract)

        def weigh(i, n=slice(0, BANK)):
            nc.vector.tensor_tensor(out=low[i][:, n], in0=low[i][:, n], in1=act[i, 0][:, n], op=ALU.mult)

        def finish(i, n=slice(0, BANK), engine=nc.gpsimd):
            s, j = divmod(i, TILES)
            engine.tensor_tensor(out=low[i][:, n], in0=low[i][:, n], in1=c_sb[s][:, j, n], op=ALU.add)
            nc.sync.dma_start(out=ov[s][:, j, n], in_=low[i][:, n])

        vcopy, scopy = nc.vector.tensor_copy, nc.scalar.copy

        def turn_half(s):
            for j in range(TILES):
                turn_h(s * TILES + j, vcopy if j % 2 == 0 else scopy)
                if s == 0 and j == TILES - 1:
                    keep_clock(1)

        def keep_both(i):
            keep_hidden(i, 1)
            keep_hidden(i, 0)

        def product_both(i):
            product(i, 1)
            product(i, 0)

        def add_both(i):
            add_up(i, 1)
            add_up(i, 0)

        lo, hi = slice(0, BANK // 2), slice(BANK // 2, BANK)

        turn_half(0)
        for t in range(PACK):
            widen(0, t)
        gate_logits(0, 0, 0, 1)
        gate_logits(0, 0, 2, 3)
        interleave_w(0, 1, vcopy)
        gate_logits(0, 1, 0)
        gate_logits(0, 1, 1)
        interleave_w(0, 0, vcopy)
        turn_half(1)
        quantize_w(0, 1)
        quantize_w(0, 0)
        order_x(0, 0, scopy)
        gate_logits(0, 1, 2)
        order_x(0, 1, scopy)
        gate_logits(0, 1, 3)
        for t in range(PACK):
            widen(1, t)
        turn_x(0, 0)
        spread_bias(1)
        spread_bias(0)
        gate_x(0, 0, 0)
        gate_x(0, 0, 1)
        interleave_w(1, 1, scopy)
        turn_x(0, 1)
        interleave_w(1, 0, scopy)
        gate_x(0, 1, 0)
        gate_x(0, 1, 1)
        quantize_w(1, 1)
        quantize_x(0, 0)
        quantize_x(0, 1)
        gate_logits(1, 0, 0)
        gate_logits(1, 0, 1)
        hidden(0)
        quantize_w(1, 0)
        keep_both(0)
        gate_logits(1, 0, 2)
        order_x(1, 0, scopy)
        gate_logits(1, 0, 3)
        order_x(1, 1, scopy)
        hidden(1)
        keep_both(1)
        product_both(0)
        product_both(1)
        turn_x(1, 0)
        add_both(0)
        add_both(1)
        gate_x(1, 0, 0)
        gate_x(1, 0, 1)
        hidden(2)
        keep_both(2)
        quantize_x(1, 0)
        for t in range(PACK):
            gate_logits(1, 1, t)
        turn_x(1, 1)
        differ(0)
        differ(1)
        weigh(0)
        weigh(1)
        gate_x(1, 1, 0)
        finish(0)
        gate_x(1, 1, 1)
        finish(1)
        hidden(3)
        keep_both(3)
        quantize_x(1, 1)
        product_both(2)
        product_both(3)
        add_both(2)
        add_both(3)
        hidden(4)
        keep_both(4)
        differ(2)
        differ(3)
        hidden(5)
        keep_both(5)
        weigh(2)
        weigh(3)
        product_both(4)
        product_both(5)
        add_both(4)
        finish(2)
        add_both(5)
        finish(3)
        hidden(6)
        keep_both(6)
        differ(4)
        differ(5)
        product_both(6)
        weigh(4)
        weigh(5)
        add_both(6)
        finish(4)
        hidden(7, (1,))
        keep_hidden(7, 1)
        product(7, 1)
        finish(5, engine=nc.vector)
        differ(6)
        hidden(7, (0,))
        weigh(6)
        add_up(7, 1)
        keep_hidden(7, 0)
        finish(6, engine=nc.vector)
        differ(7)
        product(7, 0, lo)
        product(7, 0, hi)
        add_up(7, 0, lo)
        add_up(7, 0, hi)
        weigh(7, lo)
        weigh(7, hi)
        finish(7, lo, engine=nc.vector)
        finish(7, hi, engine=nc.vector)
